import numpy as np
CORES = [1,3,5,9,11,13]
N = 6
B, TIMES = 64, 2
def setup_inputs(rng):
    return {"x": (rng.standard_normal((N, 128, B), dtype=np.float32) * (0.5 + np.abs(rng.standard_normal((1, 1, B), dtype=np.float32))) / np.float32(np.sqrt(128 * N))), "a": (rng.standard_normal((N, 128, N * 128), dtype=np.float32) / 8)}
def reference(x, a):
    X, A = x.astype(np.float64), a.astype(np.float64)
    h = X
    for _ in range(TIMES):
        h = np.stack([sum(A[r][:, 128 * j:128 * j + 128].T @ h[j] for j in range(N)) for r in range(N)])
        h = h / np.sqrt((h ** 2).sum(axis=(0, 1)))
        h = h + X
    return {"y": h.astype(np.float32)}

@@ -1,0 +1,311 @@
+from concourse.bass import DstId, RemoteDMATransfer
+from concourse.mybir import AluOpType, ActivationFunctionType
+
+B = 64
+TW = 128
+NR = 6
+AW = NR * TW
+NPOOL = 50
+
+SCRATCH = {
+    "A": ("sbuf", [128, 3 * AW], "float32"),
+    "X": ("sbuf", [128, NR * B], "float32"),
+    "U": ("sbuf", [128, NR * B], "float32"),
+    "SQ": ("sbuf", [128, NR * B], "float32"),
+    "SA": ("sbuf", [128, B], "float32"),
+    "ONES": ("sbuf", [128, 128], "float32"),
+    "STG": ("sbuf", [128, 3 * B], "float32"),
+    "LN": ("sbuf", [128, 2 * B], "float32"),
+    "WS": ("sbuf", [128, 2 * B], "float32"),
+    "WL": ("sbuf", [128, B], "float32"),
+    "N1": ("sbuf", [128, B], "float32"),
+    "PU": ("sbuf", [128, 3 * B], "float32"),
+    "V": ("sbuf", [128, 3 * B], "float32"),
+    "VQ": ("sbuf", [128, 3 * B], "float32"),
+    "VS": ("sbuf", [128, B], "float32"),
+    "SV": ("sbuf", [128, 2 * B], "float32"),
+    "S2": ("sbuf", [128, B], "float32"),
+    "N2": ("sbuf", [128, B], "float32"),
+    "D2": ("sbuf", [128, B], "float32"),
+    "TT": ("sbuf", [128, B], "float32"),
+    "Y": ("sbuf", [128, B], "float32"),
+    "pa0": ("psum", [128, 512], "float32"),
+    "pa1": ("psum", [128, 512], "float32"),
+    "pa2": ("psum", [128, 512], "float32"),
+    "pb0": ("psum", [128, 512], "float32"),
+    "pb1": ("psum", [128, 512], "float32"),
+    "pb2": ("psum", [128, 512], "float32"),
+    "ps": ("psum", [128, 512], "float32"),
+}
+SEMAPHORES = ["ldx", "lda1", "lda2", "st", "snt", "xs", "xh", "xf", "a10", "a11", "a20", "a21",
+              "uarr", "m1", "warr", "sarr"] + ["c%d" % i for i in range(NPOOL)]
+
+
+def _bits(m):
+    return [b for b in range(16) if (m >> b) & 1]
+
+
+def _mk(bs):
+    return sum(1 << b for b in bs)
+
+
+def rank_program(g, core, T, topo):
+    if T.rank_of(core) is None:
+        return
+    ADD, MUL = AluOpType.add, AluOpType.mult
+    ACT = ActivationFunctionType
+    VE, SC, PE, SY = g.vector, g.scalar, g.tensor, g.sync
+    sem = T.sem
+    cnt = [0]
+
+    def new():
+        s = sem["c%d" % cnt[0]]
+        cnt[0] += 1
+        return s
+
+    chips = []
+    for c in T.cores:
+        if topo.chip(c) not in chips:
+            chips.append(topo.chip(c))
+    loc = []
+    for ch in chips:
+        mem = [c for c in T.cores if topo.chip(c) == ch]
+        far = [c for c in T.cores if topo.chip(c) != ch]
+        hub = [c for c in mem if all(topo.may_write(c, d) for d in far)][0]
+        sats = sorted([c for c in mem if c != hub], key=lambda c: (topo.die(c) != topo.die(hub), c))
+        loc.append(sats + [hub])
+    ci = chips.index(topo.chip(core))
+    own, oth = loc[ci], loc[1 - ci]
+    base, ob = 3 * ci, 3 * (1 - ci)
+    posrank = [T.rank_of(c) for grp in loc for c in grp]
+    hub, ohub = own[2], oth[2]
+    l_me = own.index(core)
+    ro = sorted(T.rank_of(c) for c in own)
+    rf = sorted(T.rank_of(c) for c in oth)
+    near = (TW * ro[0], TW * (ro[-1] + 1))
+    farc = (TW * rf[0], TW * (rf[-1] + 1))
+
+    def blk(buf, p, n=1):
+        return buf[:, B * p:B * (p + n)]
+
+    def aslot(l, rng):
+        return T.A[:, AW * l + rng[0]:AW * l + rng[1]]
+
+    def tile(l, p):
+        j = posrank[p]
+        return T.A[:, AW * l + TW * j:AW * l + TW * (j + 1)]
+
+    def did(c):
+        rid, pid, _ = topo.addr(c)
+        return DstId(rid=rid, pnc=pid)
+
+    def send(dst, out_ap, in_ap, rsem, mask):
+        rid, pid, _ = topo.addr(dst)
+        g.remote_dma(out_ap, in_ap, rsem, sem.snt, pid, rid, mask)
+
+    SY.dma_start(blk(T.X, base + l_me), T.x[:]).then_inc(sem.ldx, 16)
+    SY.dma_start(aslot(l_me, near), T.a[:, near[0]:near[1]]).then_inc(sem.lda1, 16)
+    SC.dma_start(aslot(l_me, farc), T.a[:, farc[0]:farc[1]]).then_inc(sem.lda2, 16)
+
+    def finish(v_ap, v_sem, n_sarr):
+        s2, n2, d2, tt, yy = new(), new(), new(), new(), new()
+        VE.wait_ge(sem.sarr, n_sarr)
+        VE.tensor_tensor(T.S2[:], blk(T.SV, 0), blk(T.SV, 1), ADD).then_inc(s2, 1)
+        SC.wait_ge(s2, 1)
+        SC.activation(T.N2[:], T.S2[:], ACT.Sqrt).then_inc(n2, 1)
+        VE.wait_ge(n2, 1)
+        VE.reciprocal(T.D2[:], T.N2[:]).then_inc(d2, 1)
+        VE.wait_ge(d2, 1)
+        VE.wait_ge(v_sem, 1)
+        VE.tensor_tensor(T.TT[:], v_ap, T.D2[:], MUL).then_inc(tt, 1)
+        VE.wait_ge(tt, 1)
+        VE.wait_ge(sem.ldx, 16)
+        VE.tensor_tensor(T.Y[:], T.TT[:], blk(T.X, base + l_me), ADD).then_inc(yy, 1)
+        SY.wait_ge(yy, 1)
+        SY.dma_start(T.y[:], T.Y[:]).then_inc(sem.st, 16)
+        SY.wait_ge(sem.st, 16)
+
+    on_all = topo.mask(own[0], hub)
+    off = topo.mask(hub, ohub)
+    rest = topo.mask(hub, own[0]) & ~off
+    KO, KR = len(_bits(off)), len(_bits(rest))
+    xmask = _mk(_bits(on_all)[::2])
+    KX, KA = len(_bits(xmask)), len(_bits(on_all))
+
+    if core != hub:
+        l = l_me
+        g.wait_ge(sem.ldx, 16)
+        send(hub, blk(T.X, base + l), blk(T.X, base + l), sem.xs, xmask)
+        g.wait_ge(sem.lda1, 16)
+        send(hub, aslot(l, near), aslot(l, near), sem["a1%d" % l], on_all)
+        g.wait_ge(sem.lda2, 16)
+        send(hub, aslot(l, farc), aslot(l, farc), sem["a2%d" % l], on_all)
+        u_ap, s_ap = (blk(T.LN, 0), blk(T.LN, 1)) if l == 0 else (blk(T.LN, 1), blk(T.LN, 0))
+        km = KO if l == 0 else KR
+        n1, pu, vv = new(), new(), new()
+        SC.wait_ge(sem.m1, km)
+        SC.activation(T.N1[:], s_ap, ACT.Sqrt).then_inc(n1, 1)
+        VE.wait_ge(n1, 1)
+        VE.wait_ge(sem.m1, km)
+        VE.tensor_tensor(blk(T.PU, 0), u_ap, T.N1[:], MUL).then_inc(pu, 1)
+        VE.wait_ge(pu, 1)
+        VE.wait_ge(sem.warr, km)
+        VE.tensor_tensor(blk(T.V, 0), T.WL[:], blk(T.PU, 0), ADD).then_inc(vv, 1)
+        finish(blk(T.V, 0), vv, KR + KO)
+        g.wait_ge(sem.snt, KX + 2 * KA)
+        return
+
+    pa = [T.pa0, T.pa1, T.pa2]
+    pb = [T.pb0, T.pb1, T.pb2]
+    a1 = [sem.a10, sem.a11]
+    a2 = [sem.a20, sem.a21]
+    ones = new()
+    VE.memset(T.ONES[:], 1.0).then_inc(ones, 1)
+
+    def mm(ps, l, src, p, start, stop):
+        return PE.matmul(ps[:, 0:B], tile(l, p), blk(src, p), start, stop)
+
+    g.wait_ge(sem.ldx, 16)
+    send(ohub, blk(T.X, base + 2), blk(T.X, base + 2), sem.xh, off)
+    g.wait_ge(sem.xs, 2 * KX)
+    send(ohub, blk(T.X, base, 2), blk(T.X, base, 2), sem.xf, off)
+
+    mA = [new(), new(), new()]
+    PE.wait_ge(sem.ldx, 16)
+    PE.wait_ge(sem.lda1, 16)
+    mm(pa[2], 2, T.X, base + 2, True, False)
+    PE.wait_ge(sem.xs, 2 * KX)
+    mm(pa[2], 2, T.X, base + 0, False, False)
+    mm(pa[2], 2, T.X, base + 1, False, False)
+    PE.wait_ge(sem.xh, KO)
+    PE.wait_ge(sem.lda2, 16)
+    mm(pa[2], 2, T.X, ob + 2, False, False)
+    for l in (0, 1):
+        PE.wait_ge(a1[l], KA)
+        for q in range(3):
+            mm(pa[l], l, T.X, base + q, q == 0, False)
+    PE.wait_ge(a2[0], KA)
+    mm(pa[0], 0, T.X, ob + 2, False, False)
+    PE.wait_ge(sem.xf, KO)
+    mm(pa[2], 2, T.X, ob + 0, False, False)
+    mm(pa[2], 2, T.X, ob + 1, False, True).then_inc(mA[2], 1)
+    mm(pa[0], 0, T.X, ob + 0, False, False)
+    mm(pa[0], 0, T.X, ob + 1, False, True).then_inc(mA[0], 1)
+    PE.wait_ge(a2[1], KA)
+    mm(pa[1], 1, T.X, ob + 2, False, False)
+    mm(pa[1], 1, T.X, ob + 0, False, False)
+    mm(pa[1], 1, T.X, ob + 1, False, True).then_inc(mA[1], 1)
+
+    cu = [new(), new(), new()]
+    VE.wait_ge(mA[2], 1)
+    VE.tensor_copy(blk(T.U, base + 2), pa[2][:, 0:B]).then_inc(cu[2], 1)
+    SC.wait_ge(mA[0], 1)
+    SC.activation(blk(T.U, base + 0), pa[0][:, 0:B], ACT.Copy).then_inc(cu[0], 1)
+    VE.wait_ge(mA[1], 1)
+    VE.tensor_copy(blk(T.U, base + 1), pa[1][:, 0:B]).then_inc(cu[1], 1)
+    for s in cu:
+        g.wait_ge(s, 1)
+    send(ohub, blk(T.U, base, 3), blk(T.U, base, 3), sem.uarr, off)
+
+    for s in cu:
+        PE.wait_ge(s, 1)
+        SC.wait_ge(s, 1)
+    for l in range(3):
+        for q in range(3):
+            mm(pb[l], l, T.U, base + q, q == 0, False)
+    sqo, stga, stgb = new(), new(), new()
+    SC.activation(blk(T.SQ, base, 3), blk(T.U, base, 3), ACT.Square).then_inc(sqo, 1)
+    SC.activation(blk(T.STG, 0), blk(T.U, base + 0), ACT.Copy).then_inc(stga, 1)
+    SC.activation(blk(T.STG, 2), blk(T.U, base + 1), ACT.Copy).then_inc(stgb, 1)
+    prev = new()
+    VE.wait_ge(sqo, 1)
+    VE.tensor_tensor(T.SA[:], blk(T.SQ, base), blk(T.SQ, base + 1), ADD).then_inc(prev, 1)
+    VE.wait_ge(prev, 1)
+    prev = new()
+    VE.tensor_tensor(T.SA[:], T.SA[:], blk(T.SQ, base + 2), ADD).then_inc(prev, 1)
+
+    SC.wait_ge(sem.uarr, KO)
+    for q in range(3):
+        qs = new()
+        SC.activation(blk(T.SQ, ob + q), blk(T.U, ob + q), ACT.Square).then_inc(qs, 1)
+        VE.wait_ge(qs, 1)
+        VE.wait_ge(prev, 1)
+        prev = new()
+        VE.tensor_tensor(T.SA[:], T.SA[:], blk(T.SQ, ob + q), ADD).then_inc(prev, 1)
+    mS = new()
+    mB = [new(), new(), new()]
+    PE.wait_ge(sem.uarr, KO)
+    mm(pb[0], 0, T.U, ob + 0, False, False)
+    mm(pb[0], 0, T.U, ob + 1, False, False)
+    PE.wait_ge(prev, 1)
+    PE.wait_ge(ones, 1)
+    PE.matmul(T.ps[:, 0:B], T.ONES[:], T.SA[:], True, True).then_inc(mS, 1)
+    mm(pb[0], 0, T.U, ob + 2, False, True).then_inc(mB[0], 1)
+    for l in (1, 2):
+        mm(pb[l], l, T.U, ob + 0, False, False)
+        mm(pb[l], l, T.U, ob + 1, False, False)
+        mm(pb[l], l, T.U, ob + 2, False, True).then_inc(mB[l], 1)
+
+    stgc, n1 = new(), new()
+    N1 = pa[2][:, B:2 * B]
+    SC.wait_ge(mS, 1)
+    SC.activation(blk(T.STG, 1), T.ps[:, 0:B], ACT.Copy).then_inc(stgc, 1)
+    SC.activation(N1, T.ps[:, 0:B], ACT.Sqrt).then_inc(n1, 1)
+    for s in (stga, stgb, stgc):
+        g.wait_ge(s, 1)
+    g.remote_dma_fused([
+        RemoteDMATransfer(dst_ids=[did(own[0])], dma_engine_mask=off, remote_sem=sem.m1,
+                          src=blk(T.STG, 0, 2), dst=T.LN[:]),
+        RemoteDMATransfer(dst_ids=[did(own[1])], dma_engine_mask=rest, remote_sem=sem.m1,
+                          src=blk(T.STG, 1, 2), dst=T.LN[:]),
+    ], local_sem=sem.snt)
+
+    ws = [new(), new()]
+    for l in (0, 1):
+        VE.wait_ge(mB[l], 1)
+        VE.tensor_copy(blk(T.WS, l), pb[l][:, 0:B]).then_inc(ws[l], 1)
+        g.wait_ge(ws[l], 1)
+    g.remote_dma_fused([
+        RemoteDMATransfer(dst_ids=[did(own[0])], dma_engine_mask=off, remote_sem=sem.warr,
+                          src=blk(T.WS, 0), dst=T.WL[:]),
+        RemoteDMATransfer(dst_ids=[did(own[1])], dma_engine_mask=rest, remote_sem=sem.warr,
+                          src=blk(T.WS, 1), dst=T.WL[:]),
+    ], local_sem=sem.snt)
+
+    VE.wait_ge(n1, 1)
+    vsem, vq = [], []
+    for l in range(3):
+        pu, vv, qq = new(), new(), new()
+        VE.tensor_tensor(blk(T.PU, l), blk(T.U, base + l), N1, MUL).then_inc(pu, 1)
+        VE.wait_ge(pu, 1)
+        VE.wait_ge(mB[l], 1)
+        VE.tensor_tensor(blk(T.V, l), pb[l][:, 0:B], blk(T.PU, l), ADD).then_inc(vv, 1)
+        SC.wait_ge(vv, 1)
+        SC.activation(blk(T.VQ, l), blk(T.V, l), ACT.Square).then_inc(qq, 1)
+        vsem.append(vv)
+        vq.append(qq)
+    vs1, vs, mV, svc = new(), new(), new(), new()
+    VE.wait_ge(vq[0], 1)
+    VE.wait_ge(vq[1], 1)
+    VE.tensor_tensor(T.VS[:], blk(T.VQ, 0), blk(T.VQ, 1), ADD).then_inc(vs1, 1)
+    VE.wait_ge(vs1, 1)
+    VE.wait_ge(vq[2], 1)
+    VE.tensor_tensor(T.VS[:], T.VS[:], blk(T.VQ, 2), ADD).then_inc(vs, 1)
+    PE.wait_ge(vs, 1)
+    PE.wait_ge(stgc, 1)
+    PE.wait_ge(n1, 1)
+    PE.matmul(T.ps[:, B:2 * B], T.ONES[:], T.VS[:], True, True).then_inc(mV, 1)
+    VE.wait_ge(mV, 1)
+    VE.tensor_copy(blk(T.SV, ci), T.ps[:, B:2 * B]).then_inc(svc, 1)
+
+    g.wait_ge(svc, 1)
+    g.remote_dma_fused([
+        RemoteDMATransfer(dst_ids=[did(c) for c in oth], dma_engine_mask=off, remote_sem=sem.sarr,
+                          srcs=[blk(T.SV, ci)], dsts=[blk(T.SV, ci) for c in oth]),
+        RemoteDMATransfer(dst_ids=[did(c) for c in own[:2]], dma_engine_mask=rest, remote_sem=sem.sarr,
+                          srcs=[blk(T.SV, ci)], dsts=[blk(T.SV, ci) for c in own[:2]]),
+    ], local_sem=sem.snt)
+
+    VE.wait_ge(svc, 1)
+    finish(blk(T.V, 2), vsem[2], KO)
+    g.wait_ge(sem.snt, 3 * KO + 3 * (KO + KR))

@@ -11,9 +11,15 @@ SCRATCH = {
     "A": ("sbuf", [128, 3 * AW], "float32"),
     "X": ("sbuf", [128, NR * B], "float32"),
     "U": ("sbuf", [128, NR * B], "float32"),
-    "SQ": ("sbuf", [128, NR * B], "float32"),
+    "SQ": ("sbuf", [128, 3 * B], "float32"),
     "SA": ("sbuf", [128, B], "float32"),
     "ONES": ("sbuf", [128, 128], "float32"),
+    "SO": ("sbuf", [128, B], "float32"),
+    "SX": ("sbuf", [128, B], "float32"),
+    "RHO": ("sbuf", [128, B], "float32"),
+    "R": ("sbuf", [128, B], "float32"),
+    "Z": ("sbuf", [128, B], "float32"),
+    "F": ("sbuf", [128, B], "float32"),
     "STG": ("sbuf", [128, 3 * B], "float32"),
     "LN": ("sbuf", [128, 2 * B], "float32"),
     "WS": ("sbuf", [128, 2 * B], "float32"),
@@ -23,8 +29,7 @@ SCRATCH = {
     "V": ("sbuf", [128, 3 * B], "float32"),
     "VQ": ("sbuf", [128, 3 * B], "float32"),
     "VS": ("sbuf", [128, B], "float32"),
-    "SV": ("sbuf", [128, 2 * B], "float32"),
-    "S2": ("sbuf", [128, B], "float32"),
+    "VL": ("sbuf", [128, 2 * B], "float32"),
     "N2": ("sbuf", [128, B], "float32"),
     "D2": ("sbuf", [128, B], "float32"),
     "TT": ("sbuf", [128, B], "float32"),
@@ -38,7 +43,7 @@ SCRATCH = {
     "ps": ("psum", [128, 512], "float32"),
 }
 SEMAPHORES = ["ldx", "lda1", "lda2", "st", "snt", "xs", "xh", "xf", "a10", "a11", "a20", "a21",
-              "uarr", "m1", "warr", "sarr"] + ["c%d" % i for i in range(NPOOL)]
+              "uarr", "soarr", "m1", "warr", "svo", "svx"] + ["c%d" % i for i in range(NPOOL)]
 
 
 def _bits(m):
@@ -106,13 +111,14 @@ def rank_program(g, core, T, topo):
     SY.dma_start(blk(T.X, base + l_me), T.x[:]).then_inc(sem.ldx, 16)
     SY.dma_start(aslot(l_me, near), T.a[:, near[0]:near[1]]).then_inc(sem.lda1, 16)
     SC.dma_start(aslot(l_me, farc), T.a[:, farc[0]:farc[1]]).then_inc(sem.lda2, 16)
+    ones = new()
+    VE.memset(T.ONES[:], 1.0).then_inc(ones, 1)
+    PF = T.pa1[:, 0:B]
 
-    def finish(v_ap, v_sem, n_sarr):
-        s2, n2, d2, tt, yy = new(), new(), new(), new(), new()
-        VE.wait_ge(sem.sarr, n_sarr)
-        VE.tensor_tensor(T.S2[:], blk(T.SV, 0), blk(T.SV, 1), ADD).then_inc(s2, 1)
-        SC.wait_ge(s2, 1)
-        SC.activation(T.N2[:], T.S2[:], ACT.Sqrt).then_inc(n2, 1)
+    def finish(v_ap, v_sem, mF):
+        n2, d2, tt, yy = new(), new(), new(), new()
+        SC.wait_ge(mF, 1)
+        SC.activation(T.N2[:], PF, ACT.Sqrt).then_inc(n2, 1)
         VE.wait_ge(n2, 1)
         VE.reciprocal(T.D2[:], T.N2[:]).then_inc(d2, 1)
         VE.wait_ge(d2, 1)
@@ -142,7 +148,7 @@ def rank_program(g, core, T, topo):
         send(hub, aslot(l, farc), aslot(l, farc), sem["a2%d" % l], on_all)
         u_ap, s_ap = (blk(T.LN, 0), blk(T.LN, 1)) if l == 0 else (blk(T.LN, 1), blk(T.LN, 0))
         km = KO if l == 0 else KR
-        n1, pu, vv = new(), new(), new()
+        n1, pu, vv, mF = new(), new(), new(), new()
         SC.wait_ge(sem.m1, km)
         SC.activation(T.N1[:], s_ap, ACT.Sqrt).then_inc(n1, 1)
         VE.wait_ge(n1, 1)
@@ -151,7 +157,12 @@ def rank_program(g, core, T, topo):
         VE.wait_ge(pu, 1)
         VE.wait_ge(sem.warr, km)
         VE.tensor_tensor(blk(T.V, 0), T.WL[:], blk(T.PU, 0), ADD).then_inc(vv, 1)
-        finish(blk(T.V, 0), vv, KR + KO)
+        PE.wait_ge(ones, 1)
+        PE.wait_ge(sem.svo, KR)
+        PE.matmul(PF, T.ONES[:], blk(T.VL, ci), True, False)
+        PE.wait_ge(sem.svx, KO)
+        PE.matmul(PF, T.ONES[:], blk(T.VL, 1 - ci), False, True).then_inc(mF, 1)
+        finish(blk(T.V, 0), vv, mF)
         g.wait_ge(sem.snt, KX + 2 * KA)
         return
 
@@ -159,8 +170,6 @@ def rank_program(g, core, T, topo):
     pb = [T.pb0, T.pb1, T.pb2]
     a1 = [sem.a10, sem.a11]
     a2 = [sem.a20, sem.a21]
-    ones = new()
-    VE.memset(T.ONES[:], 1.0).then_inc(ones, 1)
 
     def mm(ps, l, src, p, start, stop):
         return PE.matmul(ps[:, 0:B], tile(l, p), blk(src, p), start, stop)
@@ -184,17 +193,13 @@ def rank_program(g, core, T, topo):
         PE.wait_ge(a1[l], KA)
         for q in range(3):
             mm(pa[l], l, T.X, base + q, q == 0, False)
-    PE.wait_ge(a2[0], KA)
-    mm(pa[0], 0, T.X, ob + 2, False, False)
+    for l in (0, 1):
+        PE.wait_ge(a2[l], KA)
+        mm(pa[l], l, T.X, ob + 2, False, False)
     PE.wait_ge(sem.xf, KO)
-    mm(pa[2], 2, T.X, ob + 0, False, False)
-    mm(pa[2], 2, T.X, ob + 1, False, True).then_inc(mA[2], 1)
-    mm(pa[0], 0, T.X, ob + 0, False, False)
-    mm(pa[0], 0, T.X, ob + 1, False, True).then_inc(mA[0], 1)
-    PE.wait_ge(a2[1], KA)
-    mm(pa[1], 1, T.X, ob + 2, False, False)
-    mm(pa[1], 1, T.X, ob + 0, False, False)
-    mm(pa[1], 1, T.X, ob + 1, False, True).then_inc(mA[1], 1)
+    for l in (2, 0, 1):
+        mm(pa[l], l, T.X, ob + 0, False, False)
+        mm(pa[l], l, T.X, ob + 1, False, True).then_inc(mA[l], 1)
 
     cu = [new(), new(), new()]
     VE.wait_ge(mA[2], 1)
@@ -210,47 +215,50 @@ def rank_program(g, core, T, topo):
     for s in cu:
         PE.wait_ge(s, 1)
         SC.wait_ge(s, 1)
-    for l in range(3):
-        for q in range(3):
-            mm(pb[l], l, T.U, base + q, q == 0, False)
-    sqo, stga, stgb = new(), new(), new()
-    SC.activation(blk(T.SQ, base, 3), blk(T.U, base, 3), ACT.Square).then_inc(sqo, 1)
-    SC.activation(blk(T.STG, 0), blk(T.U, base + 0), ACT.Copy).then_inc(stga, 1)
-    SC.activation(blk(T.STG, 2), blk(T.U, base + 1), ACT.Copy).then_inc(stgb, 1)
-    prev = new()
+    sqo, stga, stgb, sa1, sa2, mS, so, rr, rho = (new() for _ in range(9))
+    SC.activation(T.SQ[:], blk(T.U, base, 3), ACT.Square).then_inc(sqo, 1)
     VE.wait_ge(sqo, 1)
-    VE.tensor_tensor(T.SA[:], blk(T.SQ, base), blk(T.SQ, base + 1), ADD).then_inc(prev, 1)
-    VE.wait_ge(prev, 1)
-    prev = new()
-    VE.tensor_tensor(T.SA[:], T.SA[:], blk(T.SQ, base + 2), ADD).then_inc(prev, 1)
-
-    SC.wait_ge(sem.uarr, KO)
-    for q in range(3):
-        qs = new()
-        SC.activation(blk(T.SQ, ob + q), blk(T.U, ob + q), ACT.Square).then_inc(qs, 1)
-        VE.wait_ge(qs, 1)
-        VE.wait_ge(prev, 1)
-        prev = new()
-        VE.tensor_tensor(T.SA[:], T.SA[:], blk(T.SQ, ob + q), ADD).then_inc(prev, 1)
-    mS = new()
-    mB = [new(), new(), new()]
-    PE.wait_ge(sem.uarr, KO)
-    mm(pb[0], 0, T.U, ob + 0, False, False)
-    mm(pb[0], 0, T.U, ob + 1, False, False)
-    PE.wait_ge(prev, 1)
+    VE.tensor_tensor(T.SA[:], blk(T.SQ, 0), blk(T.SQ, 1), ADD).then_inc(sa1, 1)
+    VE.wait_ge(sa1, 1)
+    VE.tensor_tensor(T.SA[:], T.SA[:], blk(T.SQ, 2), ADD).then_inc(sa2, 1)
+    mm(pb[0], 0, T.U, base + 0, True, False)
+    mm(pb[0], 0, T.U, base + 1, False, False)
+    PE.wait_ge(sa2, 1)
     PE.wait_ge(ones, 1)
     PE.matmul(T.ps[:, 0:B], T.ONES[:], T.SA[:], True, True).then_inc(mS, 1)
-    mm(pb[0], 0, T.U, ob + 2, False, True).then_inc(mB[0], 1)
+    mm(pb[0], 0, T.U, base + 2, False, False)
     for l in (1, 2):
+        for q in range(3):
+            mm(pb[l], l, T.U, base + q, q == 0, False)
+    VE.wait_ge(mS, 1)
+    VE.tensor_copy(T.SO[:], T.ps[:, 0:B]).then_inc(so, 1)
+    g.wait_ge(so, 1)
+    send(ohub, T.SX[:], T.SO[:], sem.soarr, off)
+    SC.activation(blk(T.STG, 0), blk(T.U, base + 0), ACT.Copy).then_inc(stga, 1)
+    SC.activation(blk(T.STG, 2), blk(T.U, base + 1), ACT.Copy).then_inc(stgb, 1)
+    SC.wait_ge(so, 1)
+    SC.activation(T.R[:], T.SO[:], ACT.Sqrt).then_inc(rr, 1)
+    VE.wait_ge(so, 1)
+    VE.reciprocal(T.RHO[:], T.SO[:]).then_inc(rho, 1)
+
+    mB = [new(), new(), new()]
+    PE.wait_ge(sem.uarr, KO)
+    for l in range(3):
         mm(pb[l], l, T.U, ob + 0, False, False)
         mm(pb[l], l, T.U, ob + 1, False, False)
         mm(pb[l], l, T.U, ob + 2, False, True).then_inc(mB[l], 1)
 
-    stgc, n1 = new(), new()
+    stgc, zz, ff, n1 = new(), new(), new(), new()
     N1 = pa[2][:, B:2 * B]
-    SC.wait_ge(mS, 1)
-    SC.activation(blk(T.STG, 1), T.ps[:, 0:B], ACT.Copy).then_inc(stgc, 1)
-    SC.activation(N1, T.ps[:, 0:B], ACT.Sqrt).then_inc(n1, 1)
+    VE.wait_ge(sem.soarr, KO)
+    VE.tensor_tensor(blk(T.STG, 1), T.SO[:], T.SX[:], ADD).then_inc(stgc, 1)
+    VE.wait_ge(rho, 1)
+    VE.tensor_tensor(T.Z[:], T.SX[:], T.RHO[:], MUL).then_inc(zz, 1)
+    SC.wait_ge(zz, 1)
+    SC.activation(T.F[:], T.Z[:], ACT.Sqrt, bias=1.0).then_inc(ff, 1)
+    VE.wait_ge(ff, 1)
+    VE.wait_ge(rr, 1)
+    VE.tensor_tensor(N1, T.F[:], T.R[:], MUL).then_inc(n1, 1)
     for s in (stga, stgb, stgc):
         g.wait_ge(s, 1)
     g.remote_dma_fused([
@@ -259,53 +267,47 @@ def rank_program(g, core, T, topo):
         RemoteDMATransfer(dst_ids=[did(own[1])], dma_engine_mask=rest, remote_sem=sem.m1,
                           src=blk(T.STG, 1, 2), dst=T.LN[:]),
     ], local_sem=sem.snt)
+    VE.wait_ge(n1, 1)
+    pu = [new(), new(), new()]
+    for l in range(3):
+        VE.tensor_tensor(blk(T.PU, l), blk(T.U, base + l), N1, MUL).then_inc(pu[l], 1)
 
     ws = [new(), new()]
-    for l in (0, 1):
+    vsem, vq = [new(), new(), new()], [new(), new(), new()]
+    vs1, vs, mF = new(), new(), new()
+    for l in range(3):
         VE.wait_ge(mB[l], 1)
-        VE.tensor_copy(blk(T.WS, l), pb[l][:, 0:B]).then_inc(ws[l], 1)
-        g.wait_ge(ws[l], 1)
+        VE.wait_ge(pu[l], 1)
+        VE.tensor_tensor(blk(T.V, l), pb[l][:, 0:B], blk(T.PU, l), ADD).then_inc(vsem[l], 1)
+        SC.wait_ge(vsem[l], 1)
+        SC.activation(blk(T.VQ, l), blk(T.V, l), ACT.Square).then_inc(vq[l], 1)
+        if l < 2:
+            VE.tensor_copy(blk(T.WS, l), pb[l][:, 0:B]).then_inc(ws[l], 1)
+            g.wait_ge(ws[l], 1)
+        if l == 1:
+            VE.wait_ge(vq[0], 1)
+            VE.wait_ge(vq[1], 1)
+            VE.tensor_tensor(T.VS[:], blk(T.VQ, 0), blk(T.VQ, 1), ADD).then_inc(vs1, 1)
     g.remote_dma_fused([
         RemoteDMATransfer(dst_ids=[did(own[0])], dma_engine_mask=off, remote_sem=sem.warr,
                           src=blk(T.WS, 0), dst=T.WL[:]),
         RemoteDMATransfer(dst_ids=[did(own[1])], dma_engine_mask=rest, remote_sem=sem.warr,
                           src=blk(T.WS, 1), dst=T.WL[:]),
     ], local_sem=sem.snt)
-
-    VE.wait_ge(n1, 1)
-    vsem, vq = [], []
-    for l in range(3):
-        pu, vv, qq = new(), new(), new()
-        VE.tensor_tensor(blk(T.PU, l), blk(T.U, base + l), N1, MUL).then_inc(pu, 1)
-        VE.wait_ge(pu, 1)
-        VE.wait_ge(mB[l], 1)
-        VE.tensor_tensor(blk(T.V, l), pb[l][:, 0:B], blk(T.PU, l), ADD).then_inc(vv, 1)
-        SC.wait_ge(vv, 1)
-        SC.activation(blk(T.VQ, l), blk(T.V, l), ACT.Square).then_inc(qq, 1)
-        vsem.append(vv)
-        vq.append(qq)
-    vs1, vs, mV, svc = new(), new(), new(), new()
-    VE.wait_ge(vq[0], 1)
-    VE.wait_ge(vq[1], 1)
-    VE.tensor_tensor(T.VS[:], blk(T.VQ, 0), blk(T.VQ, 1), ADD).then_inc(vs1, 1)
     VE.wait_ge(vs1, 1)
     VE.wait_ge(vq[2], 1)
     VE.tensor_tensor(T.VS[:], T.VS[:], blk(T.VQ, 2), ADD).then_inc(vs, 1)
-    PE.wait_ge(vs, 1)
-    PE.wait_ge(stgc, 1)
-    PE.wait_ge(n1, 1)
-    PE.matmul(T.ps[:, B:2 * B], T.ONES[:], T.VS[:], True, True).then_inc(mV, 1)
-    VE.wait_ge(mV, 1)
-    VE.tensor_copy(blk(T.SV, ci), T.ps[:, B:2 * B]).then_inc(svc, 1)
 
-    g.wait_ge(svc, 1)
+    g.wait_ge(vs, 1)
     g.remote_dma_fused([
-        RemoteDMATransfer(dst_ids=[did(c) for c in oth], dma_engine_mask=off, remote_sem=sem.sarr,
-                          srcs=[blk(T.SV, ci)], dsts=[blk(T.SV, ci) for c in oth]),
-        RemoteDMATransfer(dst_ids=[did(c) for c in own[:2]], dma_engine_mask=rest, remote_sem=sem.sarr,
-                          srcs=[blk(T.SV, ci)], dsts=[blk(T.SV, ci) for c in own[:2]]),
+        RemoteDMATransfer(dst_ids=[did(c) for c in oth], dma_engine_mask=off, remote_sem=sem.svx,
+                          srcs=[T.VS[:]], dsts=[blk(T.VL, ci) for c in oth]),
+        RemoteDMATransfer(dst_ids=[did(c) for c in own[:2]], dma_engine_mask=rest, remote_sem=sem.svo,
+                          srcs=[T.VS[:]], dsts=[blk(T.VL, ci) for c in own[:2]]),
     ], local_sem=sem.snt)
-
-    VE.wait_ge(svc, 1)
-    finish(blk(T.V, 2), vsem[2], KO)
-    g.wait_ge(sem.snt, 3 * KO + 3 * (KO + KR))
+    PE.wait_ge(vs, 1)
+    PE.matmul(PF, T.ONES[:], T.VS[:], True, False)
+    PE.wait_ge(sem.svx, KO)
+    PE.matmul(PF, T.ONES[:], blk(T.VL, 1 - ci), False, True).then_inc(mF, 1)
+    finish(blk(T.V, 2), vsem[2], mF)
+    g.wait_ge(sem.snt, 4 * KO + 3 * (KO + KR))

from concourse.bass import DstId, RemoteDMATransfer
from concourse.mybir import AluOpType, ActivationFunctionType

B = 64
TW = 128
NR = 6
AW = NR * TW
NPOOL = 50

SCRATCH = {
    "A": ("sbuf", [128, 3 * AW], "float32"),
    "X": ("sbuf", [128, NR * B], "float32"),
    "U": ("sbuf", [128, NR * B], "float32"),
    "SQ": ("sbuf", [128, 3 * B], "float32"),
    "SA": ("sbuf", [128, B], "float32"),
    "ONES": ("sbuf", [128, 128], "float32"),
    "SO": ("sbuf", [128, B], "float32"),
    "SX": ("sbuf", [128, B], "float32"),
    "RHO": ("sbuf", [128, B], "float32"),
    "R": ("sbuf", [128, B], "float32"),
    "Z": ("sbuf", [128, B], "float32"),
    "F": ("sbuf", [128, B], "float32"),
    "STG": ("sbuf", [128, 3 * B], "float32"),
    "LN": ("sbuf", [128, 2 * B], "float32"),
    "WS": ("sbuf", [128, 2 * B], "float32"),
    "WL": ("sbuf", [128, B], "float32"),
    "N1": ("sbuf", [128, B], "float32"),
    "PU": ("sbuf", [128, 3 * B], "float32"),
    "V": ("sbuf", [128, 3 * B], "float32"),
    "VQ": ("sbuf", [128, 3 * B], "float32"),
    "VS": ("sbuf", [128, B], "float32"),
    "VL": ("sbuf", [128, 2 * B], "float32"),
    "N2": ("sbuf", [128, B], "float32"),
    "D2": ("sbuf", [128, B], "float32"),
    "TT": ("sbuf", [128, B], "float32"),
    "Y": ("sbuf", [128, B], "float32"),
    "pa0": ("psum", [128, 512], "float32"),
    "pa1": ("psum", [128, 512], "float32"),
    "pa2": ("psum", [128, 512], "float32"),
    "pb0": ("psum", [128, 512], "float32"),
    "pb1": ("psum", [128, 512], "float32"),
    "pb2": ("psum", [128, 512], "float32"),
    "ps": ("psum", [128, 512], "float32"),
}
SEMAPHORES = ["ldx", "lda1", "lda2", "st", "snt", "xs", "xh", "xf", "a10", "a11", "a20", "a21",
              "uarr", "soarr", "m1", "warr", "svo", "svx"] + ["c%d" % i for i in range(NPOOL)]


def _bits(m):
    return [b for b in range(16) if (m >> b) & 1]


def _mk(bs):
    return sum(1 << b for b in bs)


def rank_program(g, core, T, topo):
    if T.rank_of(core) is None:
        return
    ADD, MUL = AluOpType.add, AluOpType.mult
    ACT = ActivationFunctionType
    VE, SC, PE, SY = g.vector, g.scalar, g.tensor, g.sync
    sem = T.sem
    cnt = [0]

    def new():
        s = sem["c%d" % cnt[0]]
        cnt[0] += 1
        return s

    chips = []
    for c in T.cores:
        if topo.chip(c) not in chips:
            chips.append(topo.chip(c))
    loc = []
    for ch in chips:
        mem = [c for c in T.cores if topo.chip(c) == ch]
        far = [c for c in T.cores if topo.chip(c) != ch]
        hub = [c for c in mem if all(topo.may_write(c, d) for d in far)][0]
        sats = sorted([c for c in mem if c != hub], key=lambda c: (topo.die(c) != topo.die(hub), c))
        loc.append(sats + [hub])
    ci = chips.index(topo.chip(core))
    own, oth = loc[ci], loc[1 - ci]
    base, ob = 3 * ci, 3 * (1 - ci)
    posrank = [T.rank_of(c) for grp in loc for c in grp]
    hub, ohub = own[2], oth[2]
    l_me = own.index(core)
    ro = sorted(T.rank_of(c) for c in own)
    rf = sorted(T.rank_of(c) for c in oth)
    near = (TW * ro[0], TW * (ro[-1] + 1))
    farc = (TW * rf[0], TW * (rf[-1] + 1))

    def blk(buf, p, n=1):
        return buf[:, B * p:B * (p + n)]

    def aslot(l, rng):
        return T.A[:, AW * l + rng[0]:AW * l + rng[1]]

    def tile(l, p):
        j = posrank[p]
        return T.A[:, AW * l + TW * j:AW * l + TW * (j + 1)]

    def did(c):
        rid, pid, _ = topo.addr(c)
        return DstId(rid=rid, pnc=pid)

    def send(dst, out_ap, in_ap, rsem, mask):
        rid, pid, _ = topo.addr(dst)
        g.remote_dma(out_ap, in_ap, rsem, sem.snt, pid, rid, mask)

    SY.dma_start(blk(T.X, base + l_me), T.x[:]).then_inc(sem.ldx, 16)
    SY.dma_start(aslot(l_me, near), T.a[:, near[0]:near[1]]).then_inc(sem.lda1, 16)
    SC.dma_start(aslot(l_me, farc), T.a[:, farc[0]:farc[1]]).then_inc(sem.lda2, 16)
    ones = new()
    VE.memset(T.ONES[:], 1.0).then_inc(ones, 1)
    PF = T.pa1[:, 0:B]

    def finish(v_ap, v_sem, mF):
        n2, d2, tt, yy = new(), new(), new(), new()
        SC.wait_ge(mF, 1)
        SC.activation(T.N2[:], PF, ACT.Sqrt).then_inc(n2, 1)
        VE.wait_ge(n2, 1)
        VE.reciprocal(T.D2[:], T.N2[:]).then_inc(d2, 1)
        VE.wait_ge(d2, 1)
        VE.wait_ge(v_sem, 1)
        VE.tensor_tensor(T.TT[:], v_ap, T.D2[:], MUL).then_inc(tt, 1)
        VE.wait_ge(tt, 1)
        VE.wait_ge(sem.ldx, 16)
        VE.tensor_tensor(T.Y[:], T.TT[:], blk(T.X, base + l_me), ADD).then_inc(yy, 1)
        SY.wait_ge(yy, 1)
        SY.dma_start(T.y[:], T.Y[:]).then_inc(sem.st, 16)
        SY.wait_ge(sem.st, 16)

    on_all = topo.mask(own[0], hub)
    off = topo.mask(hub, ohub)
    rest = topo.mask(hub, own[0]) & ~off
    KO, KR = len(_bits(off)), len(_bits(rest))
    xmask = _mk(_bits(on_all)[::2])
    KX, KA = len(_bits(xmask)), len(_bits(on_all))

    if core != hub:
        l = l_me
        g.wait_ge(sem.ldx, 16)
        send(hub, blk(T.X, base + l), blk(T.X, base + l), sem.xs, xmask)
        g.wait_ge(sem.lda1, 16)
        send(hub, aslot(l, near), aslot(l, near), sem["a1%d" % l], on_all)
        g.wait_ge(sem.lda2, 16)
        send(hub, aslot(l, farc), aslot(l, farc), sem["a2%d" % l], on_all)
        u_ap, s_ap = (blk(T.LN, 0), blk(T.LN, 1)) if l == 0 else (blk(T.LN, 1), blk(T.LN, 0))
        km = KO if l == 0 else KR
        n1, pu, vv, mF = new(), new(), new(), new()
        SC.wait_ge(sem.m1, km)
        SC.activation(T.N1[:], s_ap, ACT.Sqrt).then_inc(n1, 1)
        VE.wait_ge(n1, 1)
        VE.wait_ge(sem.m1, km)
        VE.tensor_tensor(blk(T.PU, 0), u_ap, T.N1[:], MUL).then_inc(pu, 1)
        VE.wait_ge(pu, 1)
        VE.wait_ge(sem.warr, km)
        VE.tensor_tensor(blk(T.V, 0), T.WL[:], blk(T.PU, 0), ADD).then_inc(vv, 1)
        PE.wait_ge(ones, 1)
        PE.wait_ge(sem.svo, KR)
        PE.matmul(PF, T.ONES[:], blk(T.VL, ci), True, False)
        PE.wait_ge(sem.svx, KO)
        PE.matmul(PF, T.ONES[:], blk(T.VL, 1 - ci), False, True).then_inc(mF, 1)
        finish(blk(T.V, 0), vv, mF)
        g.wait_ge(sem.snt, KX + 2 * KA)
        return

    pa = [T.pa0, T.pa1, T.pa2]
    pb = [T.pb0, T.pb1, T.pb2]
    a1 = [sem.a10, sem.a11]
    a2 = [sem.a20, sem.a21]

    def mm(ps, l, src, p, start, stop):
        return PE.matmul(ps[:, 0:B], tile(l, p), blk(src, p), start, stop)

    g.wait_ge(sem.ldx, 16)
    send(ohub, blk(T.X, base + 2), blk(T.X, base + 2), sem.xh, off)
    g.wait_ge(sem.xs, 2 * KX)
    send(ohub, blk(T.X, base, 2), blk(T.X, base, 2), sem.xf, off)

    mA = [new(), new(), new()]
    PE.wait_ge(sem.ldx, 16)
    PE.wait_ge(sem.lda1, 16)
    mm(pa[2], 2, T.X, base + 2, True, False)
    PE.wait_ge(sem.xs, 2 * KX)
    mm(pa[2], 2, T.X, base + 0, False, False)
    mm(pa[2], 2, T.X, base + 1, False, False)
    PE.wait_ge(sem.xh, KO)
    PE.wait_ge(sem.lda2, 16)
    mm(pa[2], 2, T.X, ob + 2, False, False)
    for l in (0, 1):
        PE.wait_ge(a1[l], KA)
        for q in range(3):
            mm(pa[l], l, T.X, base + q, q == 0, False)
    for l in (0, 1):
        PE.wait_ge(a2[l], KA)
        mm(pa[l], l, T.X, ob + 2, False, False)
    PE.wait_ge(sem.xf, KO)
    for l in (2, 0, 1):
        mm(pa[l], l, T.X, ob + 0, False, False)
        mm(pa[l], l, T.X, ob + 1, False, True).then_inc(mA[l], 1)

    cu = [new(), new(), new()]
    VE.wait_ge(mA[2], 1)
    VE.tensor_copy(blk(T.U, base + 2), pa[2][:, 0:B]).then_inc(cu[2], 1)
    SC.wait_ge(mA[0], 1)
    SC.activation(blk(T.U, base + 0), pa[0][:, 0:B], ACT.Copy).then_inc(cu[0], 1)
    VE.wait_ge(mA[1], 1)
    VE.tensor_copy(blk(T.U, base + 1), pa[1][:, 0:B]).then_inc(cu[1], 1)
    for s in cu:
        g.wait_ge(s, 1)
    send(ohub, blk(T.U, base, 3), blk(T.U, base, 3), sem.uarr, off)

    for s in cu:
        PE.wait_ge(s, 1)
        SC.wait_ge(s, 1)
    sqo, stga, stgb, sa1, sa2, mS, so, rr, rho = (new() for _ in range(9))
    SC.activation(T.SQ[:], blk(T.U, base, 3), ACT.Square).then_inc(sqo, 1)
    VE.wait_ge(sqo, 1)
    VE.tensor_tensor(T.SA[:], blk(T.SQ, 0), blk(T.SQ, 1), ADD).then_inc(sa1, 1)
    VE.wait_ge(sa1, 1)
    VE.tensor_tensor(T.SA[:], T.SA[:], blk(T.SQ, 2), ADD).then_inc(sa2, 1)
    mm(pb[0], 0, T.U, base + 0, True, False)
    mm(pb[0], 0, T.U, base + 1, False, False)
    PE.wait_ge(sa2, 1)
    PE.wait_ge(ones, 1)
    PE.matmul(T.ps[:, 0:B], T.ONES[:], T.SA[:], True, True).then_inc(mS, 1)
    mm(pb[0], 0, T.U, base + 2, False, False)
    for l in (1, 2):
        for q in range(3):
            mm(pb[l], l, T.U, base + q, q == 0, False)
    VE.wait_ge(mS, 1)
    VE.tensor_copy(T.SO[:], T.ps[:, 0:B]).then_inc(so, 1)
    g.wait_ge(so, 1)
    send(ohub, T.SX[:], T.SO[:], sem.soarr, off)
    SC.activation(blk(T.STG, 0), blk(T.U, base + 0), ACT.Copy).then_inc(stga, 1)
    SC.activation(blk(T.STG, 2), blk(T.U, base + 1), ACT.Copy).then_inc(stgb, 1)
    SC.wait_ge(so, 1)
    SC.activation(T.R[:], T.SO[:], ACT.Sqrt).then_inc(rr, 1)
    VE.wait_ge(so, 1)
    VE.reciprocal(T.RHO[:], T.SO[:]).then_inc(rho, 1)

    mB = [new(), new(), new()]
    PE.wait_ge(sem.uarr, KO)
    for l in range(3):
        mm(pb[l], l, T.U, ob + 0, False, False)
        mm(pb[l], l, T.U, ob + 1, False, False)
        mm(pb[l], l, T.U, ob + 2, False, True).then_inc(mB[l], 1)

    stgc, zz, ff, n1 = new(), new(), new(), new()
    N1 = pa[2][:, B:2 * B]
    VE.wait_ge(sem.soarr, KO)
    VE.tensor_tensor(blk(T.STG, 1), T.SO[:], T.SX[:], ADD).then_inc(stgc, 1)
    VE.wait_ge(rho, 1)
    VE.tensor_tensor(T.Z[:], T.SX[:], T.RHO[:], MUL).then_inc(zz, 1)
    SC.wait_ge(zz, 1)
    SC.activation(T.F[:], T.Z[:], ACT.Sqrt, bias=1.0).then_inc(ff, 1)
    VE.wait_ge(ff, 1)
    VE.wait_ge(rr, 1)
    VE.tensor_tensor(N1, T.F[:], T.R[:], MUL).then_inc(n1, 1)
    for s in (stga, stgb, stgc):
        g.wait_ge(s, 1)
    g.remote_dma_fused([
        RemoteDMATransfer(dst_ids=[did(own[0])], dma_engine_mask=off, remote_sem=sem.m1,
                          src=blk(T.STG, 0, 2), dst=T.LN[:]),
        RemoteDMATransfer(dst_ids=[did(own[1])], dma_engine_mask=rest, remote_sem=sem.m1,
                          src=blk(T.STG, 1, 2), dst=T.LN[:]),
    ], local_sem=sem.snt)
    VE.wait_ge(n1, 1)
    pu = [new(), new(), new()]
    for l in range(3):
        VE.tensor_tensor(blk(T.PU, l), blk(T.U, base + l), N1, MUL).then_inc(pu[l], 1)

    ws = [new(), new()]
    vsem, vq = [new(), new(), new()], [new(), new(), new()]
    vs1, vs, mF = new(), new(), new()
    for l in range(3):
        VE.wait_ge(mB[l], 1)
        VE.wait_ge(pu[l], 1)
        VE.tensor_tensor(blk(T.V, l), pb[l][:, 0:B], blk(T.PU, l), ADD).then_inc(vsem[l], 1)
        SC.wait_ge(vsem[l], 1)
        SC.activation(blk(T.VQ, l), blk(T.V, l), ACT.Square).then_inc(vq[l], 1)
        if l < 2:
            VE.tensor_copy(blk(T.WS, l), pb[l][:, 0:B]).then_inc(ws[l], 1)
            g.wait_ge(ws[l], 1)
        if l == 1:
            VE.wait_ge(vq[0], 1)
            VE.wait_ge(vq[1], 1)
            VE.tensor_tensor(T.VS[:], blk(T.VQ, 0), blk(T.VQ, 1), ADD).then_inc(vs1, 1)
    g.remote_dma_fused([
        RemoteDMATransfer(dst_ids=[did(own[0])], dma_engine_mask=off, remote_sem=sem.warr,
                          src=blk(T.WS, 0), dst=T.WL[:]),
        RemoteDMATransfer(dst_ids=[did(own[1])], dma_engine_mask=rest, remote_sem=sem.warr,
                          src=blk(T.WS, 1), dst=T.WL[:]),
    ], local_sem=sem.snt)
    VE.wait_ge(vs1, 1)
    VE.wait_ge(vq[2], 1)
    VE.tensor_tensor(T.VS[:], T.VS[:], blk(T.VQ, 2), ADD).then_inc(vs, 1)

    g.wait_ge(vs, 1)
    g.remote_dma_fused([
        RemoteDMATransfer(dst_ids=[did(c) for c in oth], dma_engine_mask=off, remote_sem=sem.svx,
                          srcs=[T.VS[:]], dsts=[blk(T.VL, ci) for c in oth]),
        RemoteDMATransfer(dst_ids=[did(c) for c in own[:2]], dma_engine_mask=rest, remote_sem=sem.svo,
                          srcs=[T.VS[:]], dsts=[blk(T.VL, ci) for c in own[:2]]),
    ], local_sem=sem.snt)
    PE.wait_ge(vs, 1)
    PE.matmul(PF, T.ONES[:], T.VS[:], True, False)
    PE.wait_ge(sem.svx, KO)
    PE.matmul(PF, T.ONES[:], blk(T.VL, 1 - ci), False, True).then_inc(mF, 1)
    finish(blk(T.V, 2), vsem[2], mF)
    g.wait_ge(sem.snt, 4 * KO + 3 * (KO + KR))
